import numpy as np
import ml_dtypes


def mxq(x, axis, fmt="e4m3"):
    dtype, down = {"e4m3": (ml_dtypes.float8_e4m3fn, 7), "e5m2": (ml_dtypes.float8_e5m2, 14)}[fmt]
    v = np.moveaxis(np.asarray(x, np.float32).astype(ml_dtypes.bfloat16).astype(np.float64), axis, -1)
    blocks = v.reshape(v.shape[:-1] + (-1, 32))
    amax = np.abs(blocks).max(-1, keepdims=True)
    byte = np.maximum(np.where(amax > 0, np.frexp(amax)[1] - 1 + 127, 0) - down, 1)
    scale = np.exp2(byte - 127.0)
    codes = (blocks / scale).astype(np.float32).astype(dtype).astype(np.float64)
    return np.moveaxis((codes * scale).reshape(v.shape), -1, axis)


WIDE = False


def mx_kscale(k):
    if not WIDE:
        return np.ones(k)
    levels = np.array([10, -10, 5, -5, 0])
    if k % 512:
        return np.exp2(np.random.permutation(np.resize(levels, k // 32))).repeat(32)
    a = np.empty((k // 512, 16))
    for p in range(k // 512):
        a[p, :8] = np.random.permutation(np.resize(levels, 8))
        for g in range(8):
            far = levels[np.abs(levels - a[p, g]) >= 10]
            a[p, g + 8] = far[np.random.randint(len(far))]
    return np.exp2(a.ravel()).repeat(32)


def f64(x):
    return np.asarray(x).astype(np.float64)


def striped(idx):
    return np.tile(idx.reshape(-1, 16).T, (8, 1)).astype(np.uint16)


def unstriped(offs):
    return offs[:16].T.reshape(-1).astype(np.int64)


def relu(v):
    return np.maximum(v, 0.0)


K, T, E, C, N = 512, 768, 24, 128, 256
TOP = 4


def by_expert(wq, xq):
    return np.concatenate([wq[e].T @ xq[:, e * C:(e + 1) * C] for e in range(E)], axis=1)


def setup_inputs():
    n = np.random.standard_normal
    s = mx_kscale(K)[:, None]
    deal = np.repeat(np.arange(E), C).reshape(TOP, T)[:, np.random.permutation(T)]
    deal = np.take_along_axis(deal, np.argsort(np.random.rand(TOP, T), axis=0), axis=0)
    for _ in range(8):
        s_, t_ = np.random.permutation(T).reshape(2, -1); r = np.random.randint(TOP, size=T // 2); x, y = deal[r, s_].copy(), deal[r, t_].copy()
        ok = ~((deal[:, s_] == y).any(0) | (deal[:, t_] == x).any(0)); deal[r[ok], s_[ok]] = y[ok]; deal[r[ok], t_[ok]] = x[ok]
    order = np.lexsort((np.random.rand(TOP * T), deal.reshape(-1)))
    slot_token = order % T; pos = np.empty(TOP * T, np.int64); pos[order] = np.arange(TOP * T); pos = pos.reshape(TOP, T)
    g = np.random.uniform(0.5, 1.5, (TOP, T)); g = g / g.sum(0)
    return {
        "xT": (n((K, T)) * s).astype(np.float32),
        "w": (n((E + 1, K, N)) / np.sqrt(K) / s[None]).astype(np.float32),
        "b": (0.3 * n((N, E + 1))).astype(np.float32),
        "gate": np.stack([np.tile(r, (N, 1)) for r in g]).astype(np.float32),
        "offs": striped(slot_token),
        "pos1": striped(pos[0]),
        "pos2": striped(pos[1]),
        "pos3": striped(pos[2]),
        "pos4": striped(pos[3]),
    }


def reference(xT, w, b, gate, offs, pos1, pos2, pos3, pos4):
    idx = unstriped(offs)
    wq = mxq(f64(w), 1, "e4m3")
    xs = mxq(f64(xT), 0, "e4m3")
    ys = relu((wq[E].T @ xs) + f64(b)[:, E:])
    xq = mxq(f64(xT)[:, idx], 0, "e4m3")
    y = by_expert(wq, xq)
    y = relu(y + np.repeat(f64(b)[:, :E], C, axis=1))
    return ys + sum(f64(gate[r]) * y[:, unstriped(p)] for r, p in enumerate((pos1, pos2, pos3, pos4)))

@@ -1,0 +1,339 @@
+from contextlib import ExitStack
+
+import concourse.mybir as mybir
+from concourse.masks import make_identity
+
+K, T, E, C, N = 512, 768, 24, 128, 256
+TOP = 4
+S = E * C
+FLOPS = 2 * K * N * (S + T)
+
+F32 = mybir.dt.float32
+BF16 = mybir.dt.bfloat16
+I32 = mybir.dt.int32
+U32 = mybir.dt.uint32
+U16 = mybir.dt.uint16
+U8 = mybir.dt.uint8
+FP8X4 = mybir.dt.float8_e4m3fn_x4
+ACT = mybir.ActivationFunctionType
+ALU = mybir.AluOpType
+
+P = 128
+PACK = 4
+CHUNK = 512
+CHUNKS = S // CHUNK
+PAIRS = E // 2
+HALF_T = T // 2
+RAW_BUFS = 18
+STAGES = 9
+LATE_STAGES = 2
+CODES = 6
+MM_BANKS = 6
+PRODS = 4
+EARLY = 3
+TOK_AT = (0, 1, 4, 8, 11, 15)
+A_LEAD = 1
+IL_LAG = 1
+H1_NUM = 3
+H1_DEN = 3
+H1_CAP = 8
+EV_LAG = 3
+XS_AT = 22
+V_ITEMS = (16, 17, 18, 19, 20)
+SH_AT = 23
+BIAS_AT = 6
+IL_BF16 = 1
+IL_RING = 1
+
+
+def tile_moe_shr_lin_relu_kernel(tc, xT, w, b, gate, offs, pos1, pos2, pos3, pos4, out):
+    nc = tc.nc
+    with ExitStack() as ctx:
+        keep = ctx.enter_context(tc.tile_pool(name="keep", bufs=1))
+        ring = ctx.enter_context(tc.tile_pool(name="ring", bufs=2))
+        psum = ctx.enter_context(tc.psum_pool(name="psum", bufs=1))
+
+        offs_sb = keep.tile([P, S // 16], U16, name="offs_sb")
+        pos_sb = [keep.tile([P, T // 16], U16, name=f"pos_sb{r}") for r in range(TOP)]
+        bias = keep.tile([P, 2, 32], F32, name="bias")
+        x_raw = [keep.tile([P, 2, T], F32, name=f"x_raw{u}") for u in range(2)]
+        planes = [keep.tile([P, 2 * T], BF16, name=f"plane{u}") for u in range(2)]
+        x_codes = keep.tile([P, S + T], U32, name="x_codes", align_bytes=64)
+        x_scales = keep.tile([P, S + T], U8, name="x_scales", align_bytes=64)
+        y = [keep.tile([P, S], F32, name=f"y{h}") for h in range(2)]
+        y_shared = [keep.tile([P, T], F32, name=f"y_shared{h}") for h in range(2)]
+        ident = keep.tile([P, P], F32, name="ident")
+        stages = keep.tile([P, STAGES, 2 * P * PACK], BF16, name="stages", align_bytes=64)
+        gathered = keep.tile([P, EARLY, 2, 2 * CHUNK], BF16, name="gathered", align_bytes=64)
+        grouped = keep.tile([P, 2, PACK * CHUNK], BF16, name="grouped", align_bytes=64)
+        w_codes = keep.tile([P, CODES, 2 * P], U32, name="w_codes", align_bytes=64)
+        w_scales = keep.tile([P, CODES, 2 * P], U8, name="w_scales", align_bytes=64)
+        prods = keep.tile([P, PRODS, T], F32, name="prods")
+        turned = keep.tile([P, 4, HALF_T], F32, name="turned")
+        res = keep.tile([P, 4, HALF_T], F32, name="res")
+        banks = [psum.tile([P, 512], F32, name=f"bank{i}") for i in range(8)]
+        count = {"stage": 0, "codes": 0, "bank": 0, "grouped": 0, "prod": 0}
+
+        def turn(kind, depth):
+            count[kind] = count[kind] + 1
+            return (count[kind] - 1) % depth
+
+        def stage_slots(n):
+            if count["stage"] % STAGES + n > STAGES:
+                turn("stage", STAGES)
+            first = turn("stage", STAGES)
+            for i in range(n - 1):
+                turn("stage", STAGES)
+            return stages[:, first : first + n]
+
+        used = []
+        planes_of = {}
+
+        def cast_slot(late):
+            if late:
+                slot = used[-LATE_STAGES]
+            else:
+                slot = stage_slots(1)[:, 0]
+            used.append(slot)
+            return slot
+
+        def group_slot():
+            if IL_RING:
+                return stage_slots(2).rearrange("p a b -> p (a b)")
+            return grouped[:, turn("grouped", 2), :]
+
+        x_rows = xT.rearrange("(p u e) t -> p u e t", u=2, e=2)
+        w_raw = []
+
+        def load_w(e):
+            t = ring.tile([P, PACK, N], F32, tag="raw", bufs=RAW_BUFS, name=f"w_raw{e}")
+            nc.sync.dma_start(out=t[:], in_=w[e].rearrange("(p j) n -> p j n", j=PACK))
+            w_raw.append(t)
+
+        nc.sync.dma_start(out=x_raw[0][:], in_=x_rows[:, 0])
+        nc.sync.dma_start(offs_sb[:], offs)
+        load_w(0)
+        nc.sync.dma_start(out=x_raw[1][:], in_=x_rows[:, 1])
+        for e in range(1, E + 1):
+            load_w(e)
+            if e == BIAS_AT:
+                nc.sync.dma_start(out=bias[:, :, : E + 1], in_=b.rearrange("(h p) e -> p h e", p=P))
+        for t, src in zip(pos_sb, (pos1, pos2, pos3, pos4)):
+            nc.sync.dma_start(t[:], src)
+        gates = {}
+        for h in range(2):
+            for r in range(TOP):
+                t = ring.tile([P, T], F32, tag="raw", bufs=RAW_BUFS, name=f"gate{h}_{r}")
+                nc.sync.dma_start(out=t[:], in_=gate[r, h * P : (h + 1) * P, :])
+                gates[h, r] = t
+
+        make_identity(nc, ident[:])
+
+        def quantize(codes, scales, values):
+            nc.vector.quantize_mx(out=codes.bitcast(FP8X4), scales=scales, in_=values)
+
+        def gather(c, u):
+            if u == 0:
+                planes_of[c] = gathered[:, c] if c < EARLY else stage_slots(2)
+            lst = offs_sb[:, c * CHUNK // 16 : (c + 1) * CHUNK // 16]
+            nc.vector.tensor_copy(planes_of[c][:, u].bitcast(U32), planes[u][:].bitcast(U32).indirect(lst))
+
+        def interleave(c):
+            xi = group_slot()
+            if IL_BF16:
+                nc.vector.tensor_copy(
+                    out=xi.rearrange("p (s u e) -> p s u e", u=2, e=2),
+                    in_=planes_of[c].rearrange("p u (s e) -> p s u e", e=2),
+                )
+            else:
+                nc.vector.tensor_copy(
+                    out=xi.bitcast(I32).rearrange("p (s u) -> p s u", u=2),
+                    in_=planes_of[c].bitcast(I32).rearrange("p u s -> p s u"),
+                )
+            return xi
+
+        def quantize_x(xi, col, width):
+            quantize(x_codes[:, col : col + width], x_scales[:, col : col + width], xi[:, : PACK * width])
+
+        def cast_w(stage, i, e, h, on_vector=False):
+            dst = stage[:, i * P * PACK : (i + 1) * P * PACK].rearrange("p (c i t) -> p c t i", i=4, t=PACK)
+            src = w_raw[e][:, :, h * P : (h + 1) * P].rearrange("p t (c i) -> p c t i", i=4)
+            if on_vector:
+                nc.vector.tensor_copy(out=dst, in_=src)
+            else:
+                nc.scalar.copy(out=dst, in_=src)
+
+        def quantize_w(stage):
+            slot = turn("codes", CODES)
+            quantize(w_codes[:, slot], w_scales[:, slot], stage)
+            return slot
+
+        def matmul(acc, slot, i, x_cols):
+            wc = slice(i * P, (i + 1) * P)
+            nc.tensor.matmul_mx(
+                out=acc,
+                lhsT=w_codes[:, slot, wc].bitcast(FP8X4),
+                lhsT_scale=w_scales[:, slot, wc],
+                rhs=x_codes[:, x_cols].bitcast(FP8X4),
+                rhs_scale=x_scales[:, x_cols],
+                start=True,
+                stop=True,
+            )
+
+        def pair_casts(k, h, on_vector=False):
+            stage = stages[:, turn("stage", STAGES)]
+            cast_w(stage, 0, 2 * k, h)
+            cast_w(stage, 1, 2 * k + 1, h, on_vector)
+            return stage
+
+        def pair_products(stage, k):
+            slot = quantize_w(stage)
+            acc = banks[turn("bank", MM_BANKS)]
+            for i in range(2):
+                e = 2 * k + i
+                matmul(acc[:, i * C : (i + 1) * C], slot, i, slice(e * C, (e + 1) * C))
+            return acc
+
+        def pair_out(acc, k, h):
+            for i in range(2):
+                e = 2 * k + i
+                nc.scalar.activation(
+                    y[h][:, e * C : (e + 1) * C], acc[:, i * C : (i + 1) * C], ACT.Relu, bias=bias[:, h, e : e + 1]
+                )
+
+        def shared_tokens():
+            for t0, width in ((0, 512), (512, 256)):
+                xi = grouped[:, turn("grouped", 2), :]
+                for u in range(2):
+                    nc.vector.tensor_copy(
+                        out=xi.bitcast(I32)[:, : 2 * width].rearrange("p (s u) -> p s u", u=2)[:, :, u],
+                        in_=planes[u][:].bitcast(I32)[:, t0 : t0 + width],
+                    )
+                quantize_x(xi, S + t0, width)
+
+        def shared_products(stage):
+            slot = quantize_w(stage)
+            wide = [banks[turn("bank", MM_BANKS)] for h in range(2)]
+            narrow = banks[turn("bank", MM_BANKS)]
+            for h in range(2):
+                matmul(wide[h][:], slot, h, slice(S, S + 512))
+                matmul(narrow[:, h * 256 : (h + 1) * 256], slot, h, slice(S + 512, S + T))
+            return wide, narrow
+
+        def shared_out(wide, narrow):
+            for h in range(2):
+                nc.scalar.activation(y_shared[h][:, :512], wide[h][:], ACT.Relu, bias=bias[:, h, E : E + 1])
+                nc.scalar.activation(y_shared[h][:, 512:], narrow[:, h * 256 : (h + 1) * 256], ACT.Relu, bias=bias[:, h, E : E + 1])
+
+        def gated(h, r, lo, hi, prod):
+            nc.vector.tensor_tensor(
+                prod[:, lo:hi], y[h][:].indirect(pos_sb[r][:, lo // 16 : hi // 16]), gates[h, r][:, lo:hi], ALU.mult
+            )
+
+        def add_turned(bank, term, side, first, last):
+            for blk in range(3):
+                t0 = side * HALF_T + blk * P
+                nc.tensor.matmul(
+                    bank[:, blk * P : (blk + 1) * P],
+                    lhsT=term[:, t0 : t0 + P],
+                    rhs=ident[:],
+                    is_transpose=True,
+                    start=first and blk == 0,
+                    stop=last and blk == 2,
+                )
+
+        def turn_back(bank, back, slot):
+            nc.scalar.copy(out=turned[:, slot], in_=bank[:, :HALF_T])
+            for blk in range(3):
+                cols = slice(blk * P, (blk + 1) * P)
+                nc.tensor.transpose(back[:, cols], turned[:, slot, cols], ident[:])
+            return back[:, :HALF_T]
+
+        nc.vector.tensor_copy(out=planes[0][:].rearrange("p (t e) -> p t e", e=2), in_=x_raw[0][:].rearrange("p e t -> p t e"))
+        for c in range(EARLY):
+            gather(c, 0)
+
+        items = []
+        for k in range(PAIRS):
+            items.append((k, 0))
+            if (k + 1) * H1_NUM // H1_DEN > k * H1_NUM // H1_DEN and k < PAIRS - 1 and k * H1_NUM // H1_DEN < H1_CAP:
+                items.append((k * H1_NUM // H1_DEN, 1))
+        items.extend((k, 1) for k in range(PAIRS) if (k, 1) not in items)
+        items = items[:SH_AT] + [(PAIRS, 0)] + items[SH_AT:]
+
+        first_stages = [cast_slot(False) for h in range(2)]
+        last0 = items.index((PAIRS - 1, 0))
+        for h in range(2):
+            cast_w(first_stages[h], 0, 0, h)
+        nc.scalar.activation(planes[1][:].rearrange("p (t e) -> p t e", e=2), x_raw[1][:].rearrange("p e t -> p t e"), ACT.Copy)
+
+        sums0 = banks[6:8]
+        pending = []
+        combined = 0
+        for n, (k, h) in enumerate(items):
+            if k == 0:
+                stage = first_stages[h]
+                cast_w(stage, 1, 1, h)
+            elif k == PAIRS:
+                stage = cast_slot(n > last0)
+                for half in range(2):
+                    cast_w(stage, half, E, half)
+            else:
+                stage = cast_slot(n > last0)
+                cast_w(stage, 0, 2 * k, h)
+                cast_w(stage, 1, 2 * k + 1, h, n in V_ITEMS)
+            if n == 0:
+                gather(0, 1)
+                quantize_x(interleave(0), 0, CHUNK)
+            if k == PAIRS:
+                pending.append((shared_out, shared_products(stage)))
+            else:
+                pending.append((pair_out, (pair_products(stage, k), k, h)))
+            for c in range(1, CHUNKS):
+                if n == TOK_AT[c] + IL_LAG:
+                    quantize_x(interleave(c), c * CHUNK, CHUNK)
+            for c in range(1, CHUNKS):
+                if n == max(TOK_AT[c] - A_LEAD, 0) and c >= EARLY:
+                    gather(c, 0)
+                if n == TOK_AT[c]:
+                    gather(c, 1)
+            if n == XS_AT:
+                shared_tokens()
+            lag = 0 if (k, h) in ((PAIRS - 1, 0), (PAIRS - 1, 1)) else EV_LAG
+            while len(pending) > lag:
+                fn, args = pending[0]
+                pending = pending[1:]
+                fn(*args)
+        while pending:
+            fn, args = pending[0]
+            pending = pending[1:]
+            fn(*args)
+
+        for r in range(TOP):
+            prod = prods[:, turn("prod", PRODS)]
+            gated(0, r, 0, T, prod)
+            for side in range(2):
+                add_turned(sums0[side], prod, side, r == 0, False)
+
+        sums1 = banks[0:2]
+        for r in range(TOP - 1):
+            prod = prods[:, turn("prod", PRODS)]
+            for side in range(2):
+                gated(1, r, side * HALF_T, (side + 1) * HALF_T, prod)
+                if r == TOP - 2:
+                    add_turned(sums1[side], y_shared[1], side, False, False)
+                add_turned(sums1[side], prod, side, r == 0, r == TOP - 2)
+            if r == 0:
+                for side in range(2):
+                    add_turned(sums0[side], y_shared[0], side, False, True)
+                    back = turn_back(sums0[side], banks[2 + side], side)
+                    nc.scalar.copy(out=res[:, 2 + side], in_=back)
+                    nc.sync.dma_start(out=out[0:P, side * HALF_T : (side + 1) * HALF_T], in_=res[:, 2 + side])
+        backs = [turn_back(sums1[side], banks[4 + side], 2 + side) for side in range(2)]
+        last = prods[:, turn("prod", PRODS)]
+        for side in range(2):
+            gated(1, TOP - 1, side * HALF_T, (side + 1) * HALF_T, last)
+        for side in range(2):
+            cols = slice(side * HALF_T, (side + 1) * HALF_T)
+            nc.vector.tensor_tensor(res[:, side], last[:, cols], backs[side], ALU.add)
+            nc.sync.dma_start(out=out[P : 2 * P, cols], in_=res[:, side])

@@ -24,26 +24,29 @@ CHUNK = 512
 CHUNKS = S // CHUNK
 PAIRS = E // 2
 HALF_T = T // 2
-RAW_BUFS = 18
+RAW_BUFS = 16
 STAGES = 9
 LATE_STAGES = 2
-CODES = 6
+CODES = 4
 MM_BANKS = 6
 PRODS = 4
-EARLY = 3
-TOK_AT = (0, 1, 4, 8, 11, 15)
+EARLY = 4
+TOK_AT = (0, 2, 5, 4, 11, 15)
 A_LEAD = 1
 IL_LAG = 1
-H1_NUM = 3
-H1_DEN = 3
-H1_CAP = 8
-EV_LAG = 3
-XS_AT = 22
-V_ITEMS = (16, 17, 18, 19, 20)
-SH_AT = 23
-BIAS_AT = 6
-IL_BF16 = 1
-IL_RING = 1
+H1_NUM = 1
+H1_DEN = 1
+H1_CAP = 9
+EV_LAG = 5
+XS_AT = 12
+V_ITEMS = (8, 17, 18, 20)
+SH_AT = 21
+BIAS_AT = (12, 16, 23)
+BIAS_FROM = (0, 4, 12)
+PER_BANK = 1
+G0_AT = (23, 23, 24, 25)
+V_FIRST = (20, 21)
+IL_RING = 0
 
 
 def tile_moe_shr_lin_relu_kernel(tc, xT, w, b, gate, offs, pos1, pos2, pos3, pos4, out):
@@ -55,9 +58,14 @@ def tile_moe_shr_lin_relu_kernel(tc, xT, w, b, gate, offs, pos1, pos2, pos3, pos
 
         offs_sb = keep.tile([P, S // 16], U16, name="offs_sb")
         pos_sb = [keep.tile([P, T // 16], U16, name=f"pos_sb{r}") for r in range(TOP)]
-        bias = keep.tile([P, 2, 32], F32, name="bias")
+        bias_parts = [keep.tile([P, 2, 32], F32, name=f"bias{i}") for i in range(len(BIAS_AT))]
+
+        def bias_col(h, e):
+            part = max(i for i in range(len(BIAS_AT)) if BIAS_FROM[i] <= e)
+            return bias_parts[part][:, h, e - BIAS_FROM[part] : e - BIAS_FROM[part] + 1]
+
         x_raw = [keep.tile([P, 2, T], F32, name=f"x_raw{u}") for u in range(2)]
-        planes = [keep.tile([P, 2 * T], BF16, name=f"plane{u}") for u in range(2)]
+        planes = keep.tile([P, 2, 2 * T], BF16, name="planes")
         x_codes = keep.tile([P, S + T], U32, name="x_codes", align_bytes=64)
         x_scales = keep.tile([P, S + T], U8, name="x_scales", align_bytes=64)
         y = [keep.tile([P, S], F32, name=f"y{h}") for h in range(2)]
@@ -116,8 +124,10 @@ def tile_moe_shr_lin_relu_kernel(tc, xT, w, b, gate, offs, pos1, pos2, pos3, pos
         nc.sync.dma_start(out=x_raw[1][:], in_=x_rows[:, 1])
         for e in range(1, E + 1):
             load_w(e)
-            if e == BIAS_AT:
-                nc.sync.dma_start(out=bias[:, :, : E + 1], in_=b.rearrange("(h p) e -> p h e", p=P))
+            if e in BIAS_AT:
+                part = BIAS_AT.index(e)
+                lo, hi = (BIAS_FROM + (E + 1,))[part : part + 2]
+                nc.sync.dma_start(out=bias_parts[part][:, :, : hi - lo], in_=b.rearrange("(h p) e -> p h e", p=P)[:, :, lo:hi])
         for t, src in zip(pos_sb, (pos1, pos2, pos3, pos4)):
             nc.sync.dma_start(t[:], src)
         gates = {}
@@ -136,28 +146,25 @@ def tile_moe_shr_lin_relu_kernel(tc, xT, w, b, gate, offs, pos1, pos2, pos3, pos
             if u == 0:
                 planes_of[c] = gathered[:, c] if c < EARLY else stage_slots(2)
             lst = offs_sb[:, c * CHUNK // 16 : (c + 1) * CHUNK // 16]
-            nc.vector.tensor_copy(planes_of[c][:, u].bitcast(U32), planes[u][:].bitcast(U32).indirect(lst))
+            nc.vector.tensor_copy(planes_of[c][:, u].bitcast(U32), planes[:, u].bitcast(U32).indirect(lst))
 
-        def interleave(c):
+        def interleave(dst, pairs):
+            nc.vector.tensor_copy(
+                out=dst.bitcast(I32).rearrange("p (c i u) -> p c u i", i=2, u=2),
+                in_=pairs.bitcast(I32).rearrange("p u (c i) -> p c u i", i=2),
+            )
+
+        def group(c):
             xi = group_slot()
-            if IL_BF16:
-                nc.vector.tensor_copy(
-                    out=xi.rearrange("p (s u e) -> p s u e", u=2, e=2),
-                    in_=planes_of[c].rearrange("p u (s e) -> p s u e", e=2),
-                )
-            else:
-                nc.vector.tensor_copy(
-                    out=xi.bitcast(I32).rearrange("p (s u) -> p s u", u=2),
-                    in_=planes_of[c].bitcast(I32).rearrange("p u s -> p s u"),
-                )
+            interleave(xi, planes_of[c])
             return xi
 
         def quantize_x(xi, col, width):
             quantize(x_codes[:, col : col + width], x_scales[:, col : col + width], xi[:, : PACK * width])
 
         def cast_w(stage, i, e, h, on_vector=False):
-            dst = stage[:, i * P * PACK : (i + 1) * P * PACK].rearrange("p (c i t) -> p c t i", i=4, t=PACK)
-            src = w_raw[e][:, :, h * P : (h + 1) * P].rearrange("p t (c i) -> p c t i", i=4)
+            dst = stage[:, i * P * PACK : (i + 1) * P * PACK].rearrange("p (c i t) -> p c t i", i=2, t=PACK)
+            src = w_raw[e][:, :, h * P : (h + 1) * P].rearrange("p t (c i) -> p c t i", i=2)
             if on_vector:
                 nc.vector.tensor_copy(out=dst, in_=src)
             else:
@@ -188,7 +195,8 @@ def tile_moe_shr_lin_relu_kernel(tc, xT, w, b, gate, offs, pos1, pos2, pos3, pos
 
         def pair_products(stage, k):
             slot = quantize_w(stage)
-            acc = banks[turn("bank", MM_BANKS)]
+            place = turn("bank", MM_BANKS * PER_BANK)
+            acc = banks[place // PER_BANK][:, place % PER_BANK * 2 * C :]
             for i in range(2):
                 e = 2 * k + i
                 matmul(acc[:, i * C : (i + 1) * C], slot, i, slice(e * C, (e + 1) * C))
@@ -198,23 +206,21 @@ def tile_moe_shr_lin_relu_kernel(tc, xT, w, b, gate, offs, pos1, pos2, pos3, pos
             for i in range(2):
                 e = 2 * k + i
                 nc.scalar.activation(
-                    y[h][:, e * C : (e + 1) * C], acc[:, i * C : (i + 1) * C], ACT.Relu, bias=bias[:, h, e : e + 1]
+                    y[h][:, e * C : (e + 1) * C], acc[:, i * C : (i + 1) * C], ACT.Relu, bias=bias_col(h, e)
                 )
 
         def shared_tokens():
             for t0, width in ((0, 512), (512, 256)):
                 xi = grouped[:, turn("grouped", 2), :]
-                for u in range(2):
-                    nc.vector.tensor_copy(
-                        out=xi.bitcast(I32)[:, : 2 * width].rearrange("p (s u) -> p s u", u=2)[:, :, u],
-                        in_=planes[u][:].bitcast(I32)[:, t0 : t0 + width],
-                    )
+                interleave(xi[:, : PACK * width], planes[:, :, 2 * t0 : 2 * (t0 + width)])
                 quantize_x(xi, S + t0, width)
 
         def shared_products(stage):
             slot = quantize_w(stage)
+            count["bank"] = (count["bank"] + PER_BANK - 1) // PER_BANK
             wide = [banks[turn("bank", MM_BANKS)] for h in range(2)]
             narrow = banks[turn("bank", MM_BANKS)]
+            count["bank"] = count["bank"] * PER_BANK
             for h in range(2):
                 matmul(wide[h][:], slot, h, slice(S, S + 512))
                 matmul(narrow[:, h * 256 : (h + 1) * 256], slot, h, slice(S + 512, S + T))
@@ -222,8 +228,8 @@ def tile_moe_shr_lin_relu_kernel(tc, xT, w, b, gate, offs, pos1, pos2, pos3, pos
 
         def shared_out(wide, narrow):
             for h in range(2):
-                nc.scalar.activation(y_shared[h][:, :512], wide[h][:], ACT.Relu, bias=bias[:, h, E : E + 1])
-                nc.scalar.activation(y_shared[h][:, 512:], narrow[:, h * 256 : (h + 1) * 256], ACT.Relu, bias=bias[:, h, E : E + 1])
+                nc.scalar.activation(y_shared[h][:, :512], wide[h][:], ACT.Relu, bias=bias_col(h, E))
+                nc.scalar.activation(y_shared[h][:, 512:], narrow[:, h * 256 : (h + 1) * 256], ACT.Relu, bias=bias_col(h, E))
 
         def gated(h, r, lo, hi, prod):
             nc.vector.tensor_tensor(
@@ -249,7 +255,7 @@ def tile_moe_shr_lin_relu_kernel(tc, xT, w, b, gate, offs, pos1, pos2, pos3, pos
                 nc.tensor.transpose(back[:, cols], turned[:, slot, cols], ident[:])
             return back[:, :HALF_T]
 
-        nc.vector.tensor_copy(out=planes[0][:].rearrange("p (t e) -> p t e", e=2), in_=x_raw[0][:].rearrange("p e t -> p t e"))
+        nc.vector.tensor_copy(out=planes[:, 0].rearrange("p (c i e) -> p c e i", i=4, e=2), in_=x_raw[0][:].rearrange("p e (c i) -> p c e i", i=4))
         for c in range(EARLY):
             gather(c, 0)
 
@@ -265,9 +271,15 @@ def tile_moe_shr_lin_relu_kernel(tc, xT, w, b, gate, offs, pos1, pos2, pos3, pos
         last0 = items.index((PAIRS - 1, 0))
         for h in range(2):
             cast_w(first_stages[h], 0, 0, h)
-        nc.scalar.activation(planes[1][:].rearrange("p (t e) -> p t e", e=2), x_raw[1][:].rearrange("p e t -> p t e"), ACT.Copy)
+        nc.scalar.activation(planes[:, 1].rearrange("p (c i e) -> p c e i", i=4, e=2), x_raw[1][:].rearrange("p e (c i) -> p c e i", i=4), ACT.Copy)
 
         sums0 = banks[6:8]
+        def combine0(r):
+            prod = prods[:, turn("prod", PRODS)]
+            gated(0, r, 0, T, prod)
+            for side in range(2):
+                add_turned(sums0[side], prod, side, r == 0, False)
+
         pending = []
         combined = 0
         for n, (k, h) in enumerate(items):
@@ -280,18 +292,18 @@ def tile_moe_shr_lin_relu_kernel(tc, xT, w, b, gate, offs, pos1, pos2, pos3, pos
                     cast_w(stage, half, E, half)
             else:
                 stage = cast_slot(n > last0)
-                cast_w(stage, 0, 2 * k, h)
+                cast_w(stage, 0, 2 * k, h, n in V_FIRST)
                 cast_w(stage, 1, 2 * k + 1, h, n in V_ITEMS)
             if n == 0:
                 gather(0, 1)
-                quantize_x(interleave(0), 0, CHUNK)
+                quantize_x(group(0), 0, CHUNK)
             if k == PAIRS:
                 pending.append((shared_out, shared_products(stage)))
             else:
                 pending.append((pair_out, (pair_products(stage, k), k, h)))
             for c in range(1, CHUNKS):
                 if n == TOK_AT[c] + IL_LAG:
-                    quantize_x(interleave(c), c * CHUNK, CHUNK)
+                    quantize_x(group(c), c * CHUNK, CHUNK)
             for c in range(1, CHUNKS):
                 if n == max(TOK_AT[c] - A_LEAD, 0) and c >= EARLY:
                     gather(c, 0)
@@ -304,16 +316,15 @@ def tile_moe_shr_lin_relu_kernel(tc, xT, w, b, gate, offs, pos1, pos2, pos3, pos
                 fn, args = pending[0]
                 pending = pending[1:]
                 fn(*args)
+            while combined < TOP and n >= max(last0, G0_AT[combined]):
+                combine0(combined)
+                combined += 1
         while pending:
             fn, args = pending[0]
             pending = pending[1:]
             fn(*args)
-
-        for r in range(TOP):
-            prod = prods[:, turn("prod", PRODS)]
-            gated(0, r, 0, T, prod)
-            for side in range(2):
-                add_turned(sums0[side], prod, side, r == 0, False)
+        for r in range(combined, TOP):
+            combine0(r)
 
         sums1 = banks[0:2]
         for r in range(TOP - 1):

@@ -20,50 +20,44 @@ ALU = mybir.AluOpType
 
 P = 128
 PACK = 4
+HALF = P * PACK
 CHUNK = 512
 CHUNKS = S // CHUNK
 PAIRS = E // 2
-HALF_T = T // 2
-RAW_BUFS = 16
+SIDES = ((0, T // 2), (T // 2, T))
+SHARED_PIECES = ((0, 512), (512, 256))
+
+RAW_SLOTS = 16
 STAGES = 9
-LATE_STAGES = 2
-CODES = 4
+CODES = 3
+GROUPS = 2
 MM_BANKS = 6
 PRODS = 4
-EARLY = 4
-TOK_AT = (0, 2, 5, 4, 11, 15)
-A_LEAD = 1
-IL_LAG = 1
-H1_NUM = 1
-H1_DEN = 1
-H1_CAP = 9
-EV_LAG = 5
-XS_AT = 12
-V_ITEMS = (8, 17, 18, 20)
-SH_AT = 21
-BIAS_AT = (12, 16, 23)
-BIAS_FROM = (0, 4, 12)
-PER_BANK = 1
-G0_AT = (23, 23, 24, 25)
-V_FIRST = (20, 21)
-IL_RING = 0
+
+BOTH = 10
+JOINT_LOAD = 6
+X_SPLIT = 512
+PLANE1_AT = (0, 0, 0, 0, 2, 3)
+GROUP_AT = (0, 1, 3, 4, 6, 8)
+ON_GPSIMD = (0, 1)
+ON_VECTOR = ((17, 0), (18, 0), (18, 1), (19, 0), (19, 1), (20, 0), (23, 0), (23, 1))
+OUT_LAG = 4
+HELD_FROM = 4
+FIRST_BIAS_BEHIND = 16
+FIRST_BIAS_COUNT = 10
+LATE_LOADS = (20, 21, 0, 1, 22, 2, 23, E, 3)
 
 
 def tile_moe_shr_lin_relu_kernel(tc, xT, w, b, gate, offs, pos1, pos2, pos3, pos4, out):
     nc = tc.nc
     with ExitStack() as ctx:
         keep = ctx.enter_context(tc.tile_pool(name="keep", bufs=1))
-        ring = ctx.enter_context(tc.tile_pool(name="ring", bufs=2))
         psum = ctx.enter_context(tc.psum_pool(name="psum", bufs=1))
 
         offs_sb = keep.tile([P, S // 16], U16, name="offs_sb")
         pos_sb = [keep.tile([P, T // 16], U16, name=f"pos_sb{r}") for r in range(TOP)]
-        bias_parts = [keep.tile([P, 2, 32], F32, name=f"bias{i}") for i in range(len(BIAS_AT))]
-
-        def bias_col(h, e):
-            part = max(i for i in range(len(BIAS_AT)) if BIAS_FROM[i] <= e)
-            return bias_parts[part][:, h, e - BIAS_FROM[part] : e - BIAS_FROM[part] + 1]
-
+        bias_first = keep.tile([P, 2, 32], F32, name="bias_first")
+        bias_last = [keep.tile([P, 32], F32, name=f"bias_last{h}") for h in range(2)]
         x_raw = [keep.tile([P, 2, T], F32, name=f"x_raw{u}") for u in range(2)]
         planes = keep.tile([P, 2, 2 * T], BF16, name="planes")
         x_codes = keep.tile([P, S + T], U32, name="x_codes", align_bytes=64)
@@ -71,280 +65,261 @@ def tile_moe_shr_lin_relu_kernel(tc, xT, w, b, gate, offs, pos1, pos2, pos3, pos
         y = [keep.tile([P, S], F32, name=f"y{h}") for h in range(2)]
         y_shared = [keep.tile([P, T], F32, name=f"y_shared{h}") for h in range(2)]
         ident = keep.tile([P, P], F32, name="ident")
-        stages = keep.tile([P, STAGES, 2 * P * PACK], BF16, name="stages", align_bytes=64)
-        gathered = keep.tile([P, EARLY, 2, 2 * CHUNK], BF16, name="gathered", align_bytes=64)
-        grouped = keep.tile([P, 2, PACK * CHUNK], BF16, name="grouped", align_bytes=64)
-        w_codes = keep.tile([P, CODES, 2 * P], U32, name="w_codes", align_bytes=64)
-        w_scales = keep.tile([P, CODES, 2 * P], U8, name="w_scales", align_bytes=64)
-        prods = keep.tile([P, PRODS, T], F32, name="prods")
-        turned = keep.tile([P, 4, HALF_T], F32, name="turned")
-        res = keep.tile([P, 4, HALF_T], F32, name="res")
+        raw = keep.tile([P, RAW_SLOTS, PACK * N], F32, name="raw")
+        late = keep.tile([P, TOP * T], F32, name="late", align_bytes=64)
+        stages = keep.tile([P, STAGES, 4 * HALF], BF16, name="stages", align_bytes=64)
+        scratch = keep.tile([P, 2 * S], F32, name="scratch")
+        grouped = keep.tile([P, GROUPS, PACK * CHUNK], BF16, name="grouped", align_bytes=64)
+        w_codes = keep.tile([P, CODES, 4 * P], U32, name="w_codes", align_bytes=64)
+        w_scales = keep.tile([P, CODES, 4 * P], U8, name="w_scales", align_bytes=64)
         banks = [psum.tile([P, 512], F32, name=f"bank{i}") for i in range(8)]
-        count = {"stage": 0, "codes": 0, "bank": 0, "grouped": 0, "prod": 0}
 
-        def turn(kind, depth):
-            count[kind] = count[kind] + 1
-            return (count[kind] - 1) % depth
-
-        def stage_slots(n):
-            if count["stage"] % STAGES + n > STAGES:
-                turn("stage", STAGES)
-            first = turn("stage", STAGES)
-            for i in range(n - 1):
-                turn("stage", STAGES)
-            return stages[:, first : first + n]
-
-        used = []
-        planes_of = {}
-
-        def cast_slot(late):
-            if late:
-                slot = used[-LATE_STAGES]
-            else:
-                slot = stage_slots(1)[:, 0]
-            used.append(slot)
-            return slot
-
-        def group_slot():
-            if IL_RING:
-                return stage_slots(2).rearrange("p a b -> p (a b)")
-            return grouped[:, turn("grouped", 2), :]
+        gathered = scratch[:].bitcast(BF16).rearrange("p (c u s) -> p c u s", c=CHUNKS, u=2)
+        prods = scratch[:, : PRODS * T].rearrange("p (a t) -> p a t", t=T)
+        turned = scratch[:, PRODS * T : (PRODS + 2) * T].rearrange("p (h t) -> p h t", t=T)
+        res = scratch[:, (PRODS + 2) * T :].rearrange("p (h t) -> p h t", t=T)
+        late_stages = late[:].bitcast(BF16).rearrange("p (a b) -> p a b", b=2 * HALF)
 
         x_rows = xT.rearrange("(p u e) t -> p u e t", u=2, e=2)
-        w_raw = []
+        w_rows = w.rearrange("e (p j) n -> p e j n", j=PACK)
+        b_rows = b.rearrange("(h p) e -> p h e", p=P)
 
-        def load_w(e):
-            t = ring.tile([P, PACK, N], F32, tag="raw", bufs=RAW_BUFS, name=f"w_raw{e}")
-            nc.sync.dma_start(out=t[:], in_=w[e].rearrange("(p j) n -> p j n", j=PACK))
-            w_raw.append(t)
+        def gate_tile(h, r):
+            return late[:, r * T : (r + 1) * T] if h == 0 else raw[:, E % RAW_SLOTS + 1 + r, :T]
 
-        nc.sync.dma_start(out=x_raw[0][:], in_=x_rows[:, 0])
-        nc.sync.dma_start(offs_sb[:], offs)
-        load_w(0)
-        nc.sync.dma_start(out=x_raw[1][:], in_=x_rows[:, 1])
-        for e in range(1, E + 1):
-            load_w(e)
-            if e in BIAS_AT:
-                part = BIAS_AT.index(e)
-                lo, hi = (BIAS_FROM + (E + 1,))[part : part + 2]
-                nc.sync.dma_start(out=bias_parts[part][:, :, : hi - lo], in_=b.rearrange("(h p) e -> p h e", p=P)[:, :, lo:hi])
-        for t, src in zip(pos_sb, (pos1, pos2, pos3, pos4)):
-            nc.sync.dma_start(t[:], src)
-        gates = {}
-        for h in range(2):
+        def bias_col(h, e):
+            early = e < (FIRST_BIAS_COUNT, 2 * HELD_FROM)[h]
+            return bias_first[:, h, e : e + 1] if early else bias_last[h][:, e : e + 1]
+
+        def raw_cols(e, lo, hi):
+            slot = raw[:, e % RAW_SLOTS]
+            if 2 * BOTH <= e < E:
+                return slot[:, PACK * lo : PACK * hi].rearrange("p (j n) -> p j n", j=PACK)
+            return slot.rearrange("p (j n) -> p j n", j=PACK)[:, :, lo:hi]
+
+        def load_w(e, lo, hi):
+            nc.sync.dma_start(out=raw_cols(e, lo, hi), in_=w_rows[:, e, :, lo:hi])
+
+        def load_pair(k):
+            if JOINT_LOAD <= k < BOTH:
+                slot = 2 * k % RAW_SLOTS
+                nc.sync.dma_start(out=raw[:, slot : slot + 2], in_=w_rows[:, 2 * k : 2 * k + 2].rearrange("p e j n -> p e (j n)"))
+            else:
+                for e in (2 * k, 2 * k + 1):
+                    load_w(e, 0, N if k < BOTH else P)
+            if k == FIRST_BIAS_BEHIND // 2:
+                nc.sync.dma_start(out=bias_first[:, :, :FIRST_BIAS_COUNT], in_=b_rows[:, :, :FIRST_BIAS_COUNT])
+            if k == PAIRS - 1:
+                for h, first in enumerate((FIRST_BIAS_COUNT, 2 * HELD_FROM)):
+                    nc.sync.dma_start(out=bias_last[h][:, first : E + 1], in_=b_rows[:, h, first:])
+
+        def load_gate(h, r):
+            nc.sync.dma_start(out=gate_tile(h, r), in_=gate[r, h * P : (h + 1) * P, :])
+
+        def load_late():
+            for item in LATE_LOADS:
+                if item < TOP:
+                    nc.sync.dma_start(pos_sb[item][:], (pos1, pos2, pos3, pos4)[item])
+                    load_gate(0, item)
+                else:
+                    load_w(item, 0 if item == E else P, N)
             for r in range(TOP):
-                t = ring.tile([P, T], F32, tag="raw", bufs=RAW_BUFS, name=f"gate{h}_{r}")
-                nc.sync.dma_start(out=t[:], in_=gate[r, h * P : (h + 1) * P, :])
-                gates[h, r] = t
-
-        make_identity(nc, ident[:])
+                load_gate(1, r)
 
         def quantize(codes, scales, values):
             nc.vector.quantize_mx(out=codes.bitcast(FP8X4), scales=scales, in_=values)
 
-        def gather(c, u):
-            if u == 0:
-                planes_of[c] = gathered[:, c] if c < EARLY else stage_slots(2)
-            lst = offs_sb[:, c * CHUNK // 16 : (c + 1) * CHUNK // 16]
-            nc.vector.tensor_copy(planes_of[c][:, u].bitcast(U32), planes[:, u].bitcast(U32).indirect(lst))
+        def quantize_x(values, first, count):
+            quantize(x_codes[:, first : first + count], x_scales[:, first : first + count], values)
 
-        def interleave(dst, pairs):
-            nc.vector.tensor_copy(
-                out=dst.bitcast(I32).rearrange("p (c i u) -> p c u i", i=2, u=2),
-                in_=pairs.bitcast(I32).rearrange("p u (c i) -> p c u i", i=2),
+        def plane_views(u, lo, hi):
+            return (
+                planes[:, u, 2 * lo : 2 * hi].rearrange("p (c i e) -> p c e i", i=4, e=2),
+                x_raw[u][:, :, lo:hi].rearrange("p e (c i) -> p c e i", i=4),
             )
 
-        def group(c):
-            xi = group_slot()
-            interleave(xi, planes_of[c])
-            return xi
+        def gather(c, u):
+            offsets = offs_sb[:, c * CHUNK // 16 : (c + 1) * CHUNK // 16]
+            nc.vector.tensor_copy(gathered[:, c, u].bitcast(U32), planes[:, u].bitcast(U32).indirect(offsets))
 
-        def quantize_x(xi, col, width):
-            quantize(x_codes[:, col : col + width], x_scales[:, col : col + width], xi[:, : PACK * width])
+        def interleave(dst, words):
+            nc.vector.tensor_copy(
+                out=dst.bitcast(I32).rearrange("p (c i u) -> p c u i", i=2, u=2),
+                in_=words.bitcast(I32).rearrange("p u (c i) -> p c u i", i=2),
+            )
 
-        def cast_w(stage, i, e, h, on_vector=False):
-            dst = stage[:, i * P * PACK : (i + 1) * P * PACK].rearrange("p (c i t) -> p c t i", i=2, t=PACK)
-            src = w_raw[e][:, :, h * P : (h + 1) * P].rearrange("p t (c i) -> p c t i", i=2)
-            if on_vector:
-                nc.vector.tensor_copy(out=dst, in_=src)
+        def group_chunk(c):
+            dst = grouped[:, c % GROUPS]
+            if c in ON_GPSIMD:
+                nc.gpsimd.tensor_copy(
+                    out=dst.bitcast(I32).rearrange("p (s u) -> p s u", u=2),
+                    in_=gathered[:, c].bitcast(I32).rearrange("p u s -> p s u"),
+                )
             else:
-                nc.scalar.copy(out=dst, in_=src)
+                interleave(dst, gathered[:, c])
+            quantize_x(dst, c * CHUNK, CHUNK)
 
-        def quantize_w(stage):
-            slot = turn("codes", CODES)
-            quantize(w_codes[:, slot], w_scales[:, slot], stage)
-            return slot
+        def round_w(dst, e, halves):
+            engines = [(e, h) in ON_VECTOR for h in halves]
+            runs = [halves] if engines[0] == engines[-1] else [(h,) for h in halves]
+            for run in runs:
+                first = (run[0] - halves[0]) * HALF
+                view = dst[:, first : first + len(run) * HALF].rearrange("p (c i j) -> p c j i", i=2, j=PACK)
+                src = raw_cols(e, run[0] * P, (run[-1] + 1) * P).rearrange("p j (c i) -> p c j i", i=2)
+                if (e, run[0]) in ON_VECTOR:
+                    nc.vector.tensor_copy(out=view, in_=src)
+                else:
+                    nc.scalar.copy(out=view, in_=src)
 
-        def matmul(acc, slot, i, x_cols):
-            wc = slice(i * P, (i + 1) * P)
+        def matmul(acc, codes, scales, block, first, count):
+            w_cols, x_cols = slice(block * P, (block + 1) * P), slice(first, first + count)
             nc.tensor.matmul_mx(
                 out=acc,
-                lhsT=w_codes[:, slot, wc].bitcast(FP8X4),
-                lhsT_scale=w_scales[:, slot, wc],
+                lhsT=codes[:, w_cols].bitcast(FP8X4),
+                lhsT_scale=scales[:, w_cols],
                 rhs=x_codes[:, x_cols].bitcast(FP8X4),
                 rhs_scale=x_scales[:, x_cols],
                 start=True,
                 stop=True,
             )
 
-        def pair_casts(k, h, on_vector=False):
-            stage = stages[:, turn("stage", STAGES)]
-            cast_w(stage, 0, 2 * k, h)
-            cast_w(stage, 1, 2 * k + 1, h, on_vector)
-            return stage
+        def pair_acc(k, h, i):
+            return banks[k % MM_BANKS][:, (2 * h + i) * C : (2 * h + i + 1) * C]
 
-        def pair_products(stage, k):
-            slot = quantize_w(stage)
-            place = turn("bank", MM_BANKS * PER_BANK)
-            acc = banks[place // PER_BANK][:, place % PER_BANK * 2 * C :]
+        def pair_out(k, h):
             for i in range(2):
                 e = 2 * k + i
-                matmul(acc[:, i * C : (i + 1) * C], slot, i, slice(e * C, (e + 1) * C))
-            return acc
-
-        def pair_out(acc, k, h):
-            for i in range(2):
-                e = 2 * k + i
-                nc.scalar.activation(
-                    y[h][:, e * C : (e + 1) * C], acc[:, i * C : (i + 1) * C], ACT.Relu, bias=bias_col(h, e)
-                )
-
-        def shared_tokens():
-            for t0, width in ((0, 512), (512, 256)):
-                xi = grouped[:, turn("grouped", 2), :]
-                interleave(xi[:, : PACK * width], planes[:, :, 2 * t0 : 2 * (t0 + width)])
-                quantize_x(xi, S + t0, width)
-
-        def shared_products(stage):
-            slot = quantize_w(stage)
-            count["bank"] = (count["bank"] + PER_BANK - 1) // PER_BANK
-            wide = [banks[turn("bank", MM_BANKS)] for h in range(2)]
-            narrow = banks[turn("bank", MM_BANKS)]
-            count["bank"] = count["bank"] * PER_BANK
-            for h in range(2):
-                matmul(wide[h][:], slot, h, slice(S, S + 512))
-                matmul(narrow[:, h * 256 : (h + 1) * 256], slot, h, slice(S + 512, S + T))
-            return wide, narrow
-
-        def shared_out(wide, narrow):
-            for h in range(2):
-                nc.scalar.activation(y_shared[h][:, :512], wide[h][:], ACT.Relu, bias=bias_col(h, E))
-                nc.scalar.activation(y_shared[h][:, 512:], narrow[:, h * 256 : (h + 1) * 256], ACT.Relu, bias=bias_col(h, E))
+                nc.scalar.activation(y[h][:, e * C : (e + 1) * C], pair_acc(k, h, i), ACT.Relu, bias=bias_col(h, e))
 
         def gated(h, r, lo, hi, prod):
-            nc.vector.tensor_tensor(
-                prod[:, lo:hi], y[h][:].indirect(pos_sb[r][:, lo // 16 : hi // 16]), gates[h, r][:, lo:hi], ALU.mult
-            )
+            offsets = pos_sb[r][:, lo // 16 : hi // 16]
+            nc.vector.tensor_tensor(prod[:, lo:hi], y[h][:].indirect(offsets), gate_tile(h, r)[:, lo:hi], ALU.mult)
 
         def add_turned(bank, term, side, first, last):
-            for blk in range(3):
-                t0 = side * HALF_T + blk * P
+            lo, hi = SIDES[side]
+            for t0 in range(lo, hi, P):
                 nc.tensor.matmul(
-                    bank[:, blk * P : (blk + 1) * P],
+                    bank[:, t0 - lo : t0 - lo + P],
                     lhsT=term[:, t0 : t0 + P],
                     rhs=ident[:],
                     is_transpose=True,
-                    start=first and blk == 0,
-                    stop=last and blk == 2,
+                    start=first and t0 == lo,
+                    stop=last and t0 == hi - P,
                 )
 
-        def turn_back(bank, back, slot):
-            nc.scalar.copy(out=turned[:, slot], in_=bank[:, :HALF_T])
-            for blk in range(3):
-                cols = slice(blk * P, (blk + 1) * P)
-                nc.tensor.transpose(back[:, cols], turned[:, slot, cols], ident[:])
-            return back[:, :HALF_T]
+        def turn_back(bank, back, h, side):
+            lo, hi = SIDES[side]
+            nc.scalar.copy(out=turned[:, h, lo:hi], in_=bank[:, : hi - lo])
+            for t0 in range(lo, hi, P):
+                nc.tensor.transpose(back[:, t0 - lo : t0 - lo + P], turned[:, h, t0 : t0 + P], ident[:])
+            return back[:, : hi - lo]
 
-        nc.vector.tensor_copy(out=planes[:, 0].rearrange("p (c i e) -> p c e i", i=4, e=2), in_=x_raw[0][:].rearrange("p e (c i) -> p c e i", i=4))
-        for c in range(EARLY):
+        nc.sync.dma_start(out=x_raw[0][:], in_=x_rows[:, 0])
+        nc.sync.dma_start(offs_sb[:], offs)
+        load_w(0, 0, N)
+        nc.sync.dma_start(out=x_raw[1][:], in_=x_rows[:, 1])
+        load_w(1, 0, N)
+        for k in range(1, RAW_SLOTS // 2):
+            load_pair(k)
+        make_identity(nc, ident[:])
+
+        nc.vector.tensor_copy(*plane_views(0, 0, X_SPLIT))
+        nc.scalar.activation(*plane_views(0, X_SPLIT, T), ACT.Copy)
+        for c in range(CHUNKS):
             gather(c, 0)
+        round_w(stages[:, 0], 0, (0, 1))
+        nc.scalar.activation(*plane_views(1, 0, T), ACT.Copy)
 
-        items = []
+        pending, held = [], []
         for k in range(PAIRS):
-            items.append((k, 0))
-            if (k + 1) * H1_NUM // H1_DEN > k * H1_NUM // H1_DEN and k < PAIRS - 1 and k * H1_NUM // H1_DEN < H1_CAP:
-                items.append((k * H1_NUM // H1_DEN, 1))
-        items.extend((k, 1) for k in range(PAIRS) if (k, 1) not in items)
-        items = items[:SH_AT] + [(PAIRS, 0)] + items[SH_AT:]
+            halves = (0, 1) if k < BOTH else (0,)
+            width = 2 * len(halves)
+            stage, codes, scales = stages[:, k % STAGES], w_codes[:, k % CODES], w_scales[:, k % CODES]
+            for c in range(CHUNKS):
+                if PLANE1_AT[c] == k:
+                    gather(c, 1)
+            for i in range(2):
+                if 2 * k + i > 0:
+                    round_w(stage[:, i * len(halves) * HALF :], 2 * k + i, halves)
+            if k + RAW_SLOTS // 2 < PAIRS:
+                load_pair(k + RAW_SLOTS // 2)
+            if k == (E % RAW_SLOTS + TOP) // 2:
+                load_late()
+            for c in range(CHUNKS):
+                if GROUP_AT[c] == k:
+                    group_chunk(c)
+            quantize(codes[:, : width * P], scales[:, : width * P], stage[:, : width * HALF])
+            for h in halves:
+                for i in range(2):
+                    matmul(pair_acc(k, h, i), codes, scales, i * len(halves) + h, (2 * k + i) * C, C)
+                (held if h == 1 and k >= HELD_FROM else pending).append((k, h))
+            while len(pending) > (OUT_LAG if k < PAIRS - 1 else 0):
+                pair_out(*pending[0])
+                pending = pending[1:]
 
-        first_stages = [cast_slot(False) for h in range(2)]
-        last0 = items.index((PAIRS - 1, 0))
-        for h in range(2):
-            cast_w(first_stages[h], 0, 0, h)
-        nc.scalar.activation(planes[:, 1].rearrange("p (c i e) -> p c e i", i=4, e=2), x_raw[1][:].rearrange("p e (c i) -> p c e i", i=4), ACT.Copy)
+        for stage_of, (first, count) in zip((PAIRS - 2, PAIRS - 1), SHARED_PIECES):
+            dst = stages[:, stage_of % STAGES, : PACK * count]
+            interleave(dst, planes[:, :, 2 * first : 2 * (first + count)])
+            quantize_x(dst, S + first, count)
+        for k, h in held:
+            pair_out(k, h)
 
-        sums0 = banks[6:8]
-        def combine0(r):
-            prod = prods[:, turn("prod", PRODS)]
+        sums0 = banks[MM_BANKS:]
+
+        def combine0(r, prod):
             gated(0, r, 0, T, prod)
             for side in range(2):
                 add_turned(sums0[side], prod, side, r == 0, False)
 
-        pending = []
-        combined = 0
-        for n, (k, h) in enumerate(items):
-            if k == 0:
-                stage = first_stages[h]
-                cast_w(stage, 1, 1, h)
-            elif k == PAIRS:
-                stage = cast_slot(n > last0)
-                for half in range(2):
-                    cast_w(stage, half, E, half)
-            else:
-                stage = cast_slot(n > last0)
-                cast_w(stage, 0, 2 * k, h, n in V_FIRST)
-                cast_w(stage, 1, 2 * k + 1, h, n in V_ITEMS)
-            if n == 0:
-                gather(0, 1)
-                quantize_x(group(0), 0, CHUNK)
-            if k == PAIRS:
-                pending.append((shared_out, shared_products(stage)))
-            else:
-                pending.append((pair_out, (pair_products(stage, k), k, h)))
-            for c in range(1, CHUNKS):
-                if n == TOK_AT[c] + IL_LAG:
-                    quantize_x(group(c), c * CHUNK, CHUNK)
-            for c in range(1, CHUNKS):
-                if n == max(TOK_AT[c] - A_LEAD, 0) and c >= EARLY:
-                    gather(c, 0)
-                if n == TOK_AT[c]:
-                    gather(c, 1)
-            if n == XS_AT:
-                shared_tokens()
-            lag = 0 if (k, h) in ((PAIRS - 1, 0), (PAIRS - 1, 1)) else EV_LAG
-            while len(pending) > lag:
-                fn, args = pending[0]
-                pending = pending[1:]
-                fn(*args)
-            while combined < TOP and n >= max(last0, G0_AT[combined]):
-                combine0(combined)
-                combined += 1
-        while pending:
-            fn, args = pending[0]
-            pending = pending[1:]
-            fn(*args)
-        for r in range(combined, TOP):
-            combine0(r)
+        def late_pair(k):
+            stage, codes, scales = late_stages[:, k - BOTH], w_codes[:, k % CODES, 2 * P :], w_scales[:, k % CODES, 2 * P :]
+            for i in range(2):
+                round_w(stage[:, i * HALF :], 2 * k + i, (1,))
+            quantize(codes, scales, stage)
+            for i in range(2):
+                matmul(pair_acc(k, 1, i), codes, scales, i, (2 * k + i) * C, C)
 
-        sums1 = banks[0:2]
+        combine0(0, prods[:, 0])
+        late_pair(BOTH)
+        combine0(1, prods[:, 1])
+        late_pair(BOTH + 1)
+        shared_stage = late_stages[:, PAIRS - BOTH]
+        round_w(shared_stage, E, (0, 1))
+        for k in range(BOTH, PAIRS):
+            pair_out(k, 1)
+        combine0(2, prods[:, 2])
+        late_end = (PAIRS - BOTH) * HALF
+        combine0(3, late[:, late_end - T : late_end])
+
+        codes, scales = w_codes[:, PAIRS % CODES, : 2 * P], w_scales[:, PAIRS % CODES, : 2 * P]
+        quantize(codes, scales, shared_stage)
+        wide, narrow = (count for first, count in SHARED_PIECES)
+        for h in range(2):
+            matmul(banks[h][:], codes, scales, h, S, wide)
+            matmul(banks[2][:, h * narrow : (h + 1) * narrow], codes, scales, h, S + wide, narrow)
+        for h in range(2):
+            nc.scalar.activation(y_shared[h][:, :wide], banks[h][:], ACT.Relu, bias=bias_col(h, E))
+            nc.scalar.activation(y_shared[h][:, wide:], banks[2][:, h * narrow : (h + 1) * narrow], ACT.Relu, bias=bias_col(h, E))
+
+        sums1 = banks[:2]
         for r in range(TOP - 1):
-            prod = prods[:, turn("prod", PRODS)]
+            prod = prods[:, (TOP - 1 + r) % PRODS]
             for side in range(2):
-                gated(1, r, side * HALF_T, (side + 1) * HALF_T, prod)
-                if r == TOP - 2:
+                gated(1, r, *SIDES[side], prod)
+                if r == 1:
                     add_turned(sums1[side], y_shared[1], side, False, False)
                 add_turned(sums1[side], prod, side, r == 0, r == TOP - 2)
             if r == 0:
                 for side in range(2):
                     add_turned(sums0[side], y_shared[0], side, False, True)
-                    back = turn_back(sums0[side], banks[2 + side], side)
-                    nc.scalar.copy(out=res[:, 2 + side], in_=back)
-                    nc.sync.dma_start(out=out[0:P, side * HALF_T : (side + 1) * HALF_T], in_=res[:, 2 + side])
-        backs = [turn_back(sums1[side], banks[4 + side], 2 + side) for side in range(2)]
-        last = prods[:, turn("prod", PRODS)]
+                    cols = slice(*SIDES[side])
+                    nc.scalar.copy(out=res[:, 0, cols], in_=turn_back(sums0[side], banks[2 + side], 0, side))
+                    nc.sync.dma_start(out=out[:P, cols], in_=res[:, 0, cols])
+        backs = [turn_back(sums1[side], banks[4 + side], 1, side) for side in range(2)]
+        last = prods[:, (2 * TOP - 2) % PRODS]
         for side in range(2):
-            gated(1, TOP - 1, side * HALF_T, (side + 1) * HALF_T, last)
+            gated(1, TOP - 1, *SIDES[side], last)
         for side in range(2):
-            cols = slice(side * HALF_T, (side + 1) * HALF_T)
-            nc.vector.tensor_tensor(res[:, side], last[:, cols], backs[side], ALU.add)
-            nc.sync.dma_start(out=out[P : 2 * P, cols], in_=res[:, side])
+            cols = slice(*SIDES[side])
+            nc.vector.tensor_tensor(res[:, 1, cols], last[:, cols], backs[side], ALU.add)
+            nc.sync.dma_start(out=out[P:, cols], in_=res[:, 1, cols])

from contextlib import ExitStack

import concourse.mybir as mybir
from concourse.masks import make_identity

K, T, E, C, N = 512, 768, 24, 128, 256
TOP = 4
S = E * C
FLOPS = 2 * K * N * (S + T)

F32 = mybir.dt.float32
BF16 = mybir.dt.bfloat16
I32 = mybir.dt.int32
U32 = mybir.dt.uint32
U16 = mybir.dt.uint16
U8 = mybir.dt.uint8
FP8X4 = mybir.dt.float8_e4m3fn_x4
ACT = mybir.ActivationFunctionType
ALU = mybir.AluOpType

P = 128
PACK = 4
HALF = P * PACK
CHUNK = 512
CHUNKS = S // CHUNK
PAIRS = E // 2
SIDES = ((0, T // 2), (T // 2, T))
SHARED_PIECES = ((0, 512), (512, 256))

RAW_SLOTS = 16
STAGES = 9
CODES = 3
GROUPS = 2
MM_BANKS = 6
PRODS = 4

BOTH = 10
JOINT_LOAD = 6
X_SPLIT = 512
PLANE1_AT = (0, 0, 0, 0, 2, 3)
GROUP_AT = (0, 1, 3, 4, 6, 8)
ON_GPSIMD = (0, 1)
ON_VECTOR = ((17, 0), (18, 0), (18, 1), (19, 0), (19, 1), (20, 0), (23, 0), (23, 1))
OUT_LAG = 4
HELD_FROM = 4
FIRST_BIAS_BEHIND = 16
FIRST_BIAS_COUNT = 10
LATE_LOADS = (20, 21, 0, 1, 22, 2, 23, E, 3)


def tile_moe_shr_lin_relu_kernel(tc, xT, w, b, gate, offs, pos1, pos2, pos3, pos4, out):
    nc = tc.nc
    with ExitStack() as ctx:
        keep = ctx.enter_context(tc.tile_pool(name="keep", bufs=1))
        psum = ctx.enter_context(tc.psum_pool(name="psum", bufs=1))

        offs_sb = keep.tile([P, S // 16], U16, name="offs_sb")
        pos_sb = [keep.tile([P, T // 16], U16, name=f"pos_sb{r}") for r in range(TOP)]
        bias_first = keep.tile([P, 2, 32], F32, name="bias_first")
        bias_last = [keep.tile([P, 32], F32, name=f"bias_last{h}") for h in range(2)]
        x_raw = [keep.tile([P, 2, T], F32, name=f"x_raw{u}") for u in range(2)]
        planes = keep.tile([P, 2, 2 * T], BF16, name="planes")
        x_codes = keep.tile([P, S + T], U32, name="x_codes", align_bytes=64)
        x_scales = keep.tile([P, S + T], U8, name="x_scales", align_bytes=64)
        y = [keep.tile([P, S], F32, name=f"y{h}") for h in range(2)]
        y_shared = [keep.tile([P, T], F32, name=f"y_shared{h}") for h in range(2)]
        ident = keep.tile([P, P], F32, name="ident")
        raw = keep.tile([P, RAW_SLOTS, PACK * N], F32, name="raw")
        late = keep.tile([P, TOP * T], F32, name="late", align_bytes=64)
        stages = keep.tile([P, STAGES, 4 * HALF], BF16, name="stages", align_bytes=64)
        scratch = keep.tile([P, 2 * S], F32, name="scratch")
        grouped = keep.tile([P, GROUPS, PACK * CHUNK], BF16, name="grouped", align_bytes=64)
        w_codes = keep.tile([P, CODES, 4 * P], U32, name="w_codes", align_bytes=64)
        w_scales = keep.tile([P, CODES, 4 * P], U8, name="w_scales", align_bytes=64)
        banks = [psum.tile([P, 512], F32, name=f"bank{i}") for i in range(8)]

        gathered = scratch[:].bitcast(BF16).rearrange("p (c u s) -> p c u s", c=CHUNKS, u=2)
        prods = scratch[:, : PRODS * T].rearrange("p (a t) -> p a t", t=T)
        turned = scratch[:, PRODS * T : (PRODS + 2) * T].rearrange("p (h t) -> p h t", t=T)
        res = scratch[:, (PRODS + 2) * T :].rearrange("p (h t) -> p h t", t=T)
        late_stages = late[:].bitcast(BF16).rearrange("p (a b) -> p a b", b=2 * HALF)

        x_rows = xT.rearrange("(p u e) t -> p u e t", u=2, e=2)
        w_rows = w.rearrange("e (p j) n -> p e j n", j=PACK)
        b_rows = b.rearrange("(h p) e -> p h e", p=P)

        def gate_tile(h, r):
            return late[:, r * T : (r + 1) * T] if h == 0 else raw[:, E % RAW_SLOTS + 1 + r, :T]

        def bias_col(h, e):
            early = e < (FIRST_BIAS_COUNT, 2 * HELD_FROM)[h]
            return bias_first[:, h, e : e + 1] if early else bias_last[h][:, e : e + 1]

        def raw_cols(e, lo, hi):
            slot = raw[:, e % RAW_SLOTS]
            if 2 * BOTH <= e < E:
                return slot[:, PACK * lo : PACK * hi].rearrange("p (j n) -> p j n", j=PACK)
            return slot.rearrange("p (j n) -> p j n", j=PACK)[:, :, lo:hi]

        def load_w(e, lo, hi):
            nc.sync.dma_start(out=raw_cols(e, lo, hi), in_=w_rows[:, e, :, lo:hi])

        def load_pair(k):
            if JOINT_LOAD <= k < BOTH:
                slot = 2 * k % RAW_SLOTS
                nc.sync.dma_start(out=raw[:, slot : slot + 2], in_=w_rows[:, 2 * k : 2 * k + 2].rearrange("p e j n -> p e (j n)"))
            else:
                for e in (2 * k, 2 * k + 1):
                    load_w(e, 0, N if k < BOTH else P)
            if k == FIRST_BIAS_BEHIND // 2:
                nc.sync.dma_start(out=bias_first[:, :, :FIRST_BIAS_COUNT], in_=b_rows[:, :, :FIRST_BIAS_COUNT])
            if k == PAIRS - 1:
                for h, first in enumerate((FIRST_BIAS_COUNT, 2 * HELD_FROM)):
                    nc.sync.dma_start(out=bias_last[h][:, first : E + 1], in_=b_rows[:, h, first:])

        def load_gate(h, r):
            nc.sync.dma_start(out=gate_tile(h, r), in_=gate[r, h * P : (h + 1) * P, :])

        def load_late():
            for item in LATE_LOADS:
                if item < TOP:
                    nc.sync.dma_start(pos_sb[item][:], (pos1, pos2, pos3, pos4)[item])
                    load_gate(0, item)
                else:
                    load_w(item, 0 if item == E else P, N)
            for r in range(TOP):
                load_gate(1, r)

        def quantize(codes, scales, values):
            nc.vector.quantize_mx(out=codes.bitcast(FP8X4), scales=scales, in_=values)

        def quantize_x(values, first, count):
            quantize(x_codes[:, first : first + count], x_scales[:, first : first + count], values)

        def plane_views(u, lo, hi):
            return (
                planes[:, u, 2 * lo : 2 * hi].rearrange("p (c i e) -> p c e i", i=4, e=2),
                x_raw[u][:, :, lo:hi].rearrange("p e (c i) -> p c e i", i=4),
            )

        def gather(c, u):
            offsets = offs_sb[:, c * CHUNK // 16 : (c + 1) * CHUNK // 16]
            nc.vector.tensor_copy(gathered[:, c, u].bitcast(U32), planes[:, u].bitcast(U32).indirect(offsets))

        def interleave(dst, words):
            nc.vector.tensor_copy(
                out=dst.bitcast(I32).rearrange("p (c i u) -> p c u i", i=2, u=2),
                in_=words.bitcast(I32).rearrange("p u (c i) -> p c u i", i=2),
            )

        def group_chunk(c):
            dst = grouped[:, c % GROUPS]
            if c in ON_GPSIMD:
                nc.gpsimd.tensor_copy(
                    out=dst.bitcast(I32).rearrange("p (s u) -> p s u", u=2),
                    in_=gathered[:, c].bitcast(I32).rearrange("p u s -> p s u"),
                )
            else:
                interleave(dst, gathered[:, c])
            quantize_x(dst, c * CHUNK, CHUNK)

        def round_w(dst, e, halves):
            engines = [(e, h) in ON_VECTOR for h in halves]
            runs = [halves] if engines[0] == engines[-1] else [(h,) for h in halves]
            for run in runs:
                first = (run[0] - halves[0]) * HALF
                view = dst[:, first : first + len(run) * HALF].rearrange("p (c i j) -> p c j i", i=2, j=PACK)
                src = raw_cols(e, run[0] * P, (run[-1] + 1) * P).rearrange("p j (c i) -> p c j i", i=2)
                if (e, run[0]) in ON_VECTOR:
                    nc.vector.tensor_copy(out=view, in_=src)
                else:
                    nc.scalar.copy(out=view, in_=src)

        def matmul(acc, codes, scales, block, first, count):
            w_cols, x_cols = slice(block * P, (block + 1) * P), slice(first, first + count)
            nc.tensor.matmul_mx(
                out=acc,
                lhsT=codes[:, w_cols].bitcast(FP8X4),
                lhsT_scale=scales[:, w_cols],
                rhs=x_codes[:, x_cols].bitcast(FP8X4),
                rhs_scale=x_scales[:, x_cols],
                start=True,
                stop=True,
            )

        def pair_acc(k, h, i):
            return banks[k % MM_BANKS][:, (2 * h + i) * C : (2 * h + i + 1) * C]

        def pair_out(k, h):
            for i in range(2):
                e = 2 * k + i
                nc.scalar.activation(y[h][:, e * C : (e + 1) * C], pair_acc(k, h, i), ACT.Relu, bias=bias_col(h, e))

        def gated(h, r, lo, hi, prod):
            offsets = pos_sb[r][:, lo // 16 : hi // 16]
            nc.vector.tensor_tensor(prod[:, lo:hi], y[h][:].indirect(offsets), gate_tile(h, r)[:, lo:hi], ALU.mult)

        def add_turned(bank, term, side, first, last):
            lo, hi = SIDES[side]
            for t0 in range(lo, hi, P):
                nc.tensor.matmul(
                    bank[:, t0 - lo : t0 - lo + P],
                    lhsT=term[:, t0 : t0 + P],
                    rhs=ident[:],
                    is_transpose=True,
                    start=first and t0 == lo,
                    stop=last and t0 == hi - P,
                )

        def turn_back(bank, back, h, side):
            lo, hi = SIDES[side]
            nc.scalar.copy(out=turned[:, h, lo:hi], in_=bank[:, : hi - lo])
            for t0 in range(lo, hi, P):
                nc.tensor.transpose(back[:, t0 - lo : t0 - lo + P], turned[:, h, t0 : t0 + P], ident[:])
            return back[:, : hi - lo]

        nc.sync.dma_start(out=x_raw[0][:], in_=x_rows[:, 0])
        nc.sync.dma_start(offs_sb[:], offs)
        load_w(0, 0, N)
        nc.sync.dma_start(out=x_raw[1][:], in_=x_rows[:, 1])
        load_w(1, 0, N)
        for k in range(1, RAW_SLOTS // 2):
            load_pair(k)
        make_identity(nc, ident[:])

        nc.vector.tensor_copy(*plane_views(0, 0, X_SPLIT))
        nc.scalar.activation(*plane_views(0, X_SPLIT, T), ACT.Copy)
        for c in range(CHUNKS):
            gather(c, 0)
        round_w(stages[:, 0], 0, (0, 1))
        nc.scalar.activation(*plane_views(1, 0, T), ACT.Copy)

        pending, held = [], []
        for k in range(PAIRS):
            halves = (0, 1) if k < BOTH else (0,)
            width = 2 * len(halves)
            stage, codes, scales = stages[:, k % STAGES], w_codes[:, k % CODES], w_scales[:, k % CODES]
            for c in range(CHUNKS):
                if PLANE1_AT[c] == k:
                    gather(c, 1)
            for i in range(2):
                if 2 * k + i > 0:
                    round_w(stage[:, i * len(halves) * HALF :], 2 * k + i, halves)
            if k + RAW_SLOTS // 2 < PAIRS:
                load_pair(k + RAW_SLOTS // 2)
            if k == (E % RAW_SLOTS + TOP) // 2:
                load_late()
            for c in range(CHUNKS):
                if GROUP_AT[c] == k:
                    group_chunk(c)
            quantize(codes[:, : width * P], scales[:, : width * P], stage[:, : width * HALF])
            for h in halves:
                for i in range(2):
                    matmul(pair_acc(k, h, i), codes, scales, i * len(halves) + h, (2 * k + i) * C, C)
                (held if h == 1 and k >= HELD_FROM else pending).append((k, h))
            while len(pending) > (OUT_LAG if k < PAIRS - 1 else 0):
                pair_out(*pending[0])
                pending = pending[1:]

        for stage_of, (first, count) in zip((PAIRS - 2, PAIRS - 1), SHARED_PIECES):
            dst = stages[:, stage_of % STAGES, : PACK * count]
            interleave(dst, planes[:, :, 2 * first : 2 * (first + count)])
            quantize_x(dst, S + first, count)
        for k, h in held:
            pair_out(k, h)

        sums0 = banks[MM_BANKS:]

        def combine0(r, prod):
            gated(0, r, 0, T, prod)
            for side in range(2):
                add_turned(sums0[side], prod, side, r == 0, False)

        def late_pair(k):
            stage, codes, scales = late_stages[:, k - BOTH], w_codes[:, k % CODES, 2 * P :], w_scales[:, k % CODES, 2 * P :]
            for i in range(2):
                round_w(stage[:, i * HALF :], 2 * k + i, (1,))
            quantize(codes, scales, stage)
            for i in range(2):
                matmul(pair_acc(k, 1, i), codes, scales, i, (2 * k + i) * C, C)

        combine0(0, prods[:, 0])
        late_pair(BOTH)
        combine0(1, prods[:, 1])
        late_pair(BOTH + 1)
        shared_stage = late_stages[:, PAIRS - BOTH]
        round_w(shared_stage, E, (0, 1))
        for k in range(BOTH, PAIRS):
            pair_out(k, 1)
        combine0(2, prods[:, 2])
        late_end = (PAIRS - BOTH) * HALF
        combine0(3, late[:, late_end - T : late_end])

        codes, scales = w_codes[:, PAIRS % CODES, : 2 * P], w_scales[:, PAIRS % CODES, : 2 * P]
        quantize(codes, scales, shared_stage)
        wide, narrow = (count for first, count in SHARED_PIECES)
        for h in range(2):
            matmul(banks[h][:], codes, scales, h, S, wide)
            matmul(banks[2][:, h * narrow : (h + 1) * narrow], codes, scales, h, S + wide, narrow)
        for h in range(2):
            nc.scalar.activation(y_shared[h][:, :wide], banks[h][:], ACT.Relu, bias=bias_col(h, E))
            nc.scalar.activation(y_shared[h][:, wide:], banks[2][:, h * narrow : (h + 1) * narrow], ACT.Relu, bias=bias_col(h, E))

        sums1 = banks[:2]
        for r in range(TOP - 1):
            prod = prods[:, (TOP - 1 + r) % PRODS]
            for side in range(2):
                gated(1, r, *SIDES[side], prod)
                if r == 1:
                    add_turned(sums1[side], y_shared[1], side, False, False)
                add_turned(sums1[side], prod, side, r == 0, r == TOP - 2)
            if r == 0:
                for side in range(2):
                    add_turned(sums0[side], y_shared[0], side, False, True)
                    cols = slice(*SIDES[side])
                    nc.scalar.copy(out=res[:, 0, cols], in_=turn_back(sums0[side], banks[2 + side], 0, side))
                    nc.sync.dma_start(out=out[:P, cols], in_=res[:, 0, cols])
        backs = [turn_back(sums1[side], banks[4 + side], 1, side) for side in range(2)]
        last = prods[:, (2 * TOP - 2) % PRODS]
        for side in range(2):
            gated(1, TOP - 1, *SIDES[side], last)
        for side in range(2):
            cols = slice(*SIDES[side])
            nc.vector.tensor_tensor(res[:, 1, cols], last[:, cols], backs[side], ALU.add)
            nc.sync.dma_start(out=out[P:, cols], in_=res[:, 1, cols])
